import numpy as np
import ml_dtypes


def mxq(x, axis, fmt="e4m3"):
    dtype, down = {"e4m3": (ml_dtypes.float8_e4m3fn, 7), "e5m2": (ml_dtypes.float8_e5m2, 14)}[fmt]
    v = np.moveaxis(np.asarray(x, np.float32).astype(ml_dtypes.bfloat16).astype(np.float64), axis, -1)
    blocks = v.reshape(v.shape[:-1] + (-1, 32))
    amax = np.abs(blocks).max(-1, keepdims=True)
    byte = np.maximum(np.where(amax > 0, np.frexp(amax)[1] - 1 + 127, 0) - down, 1)
    scale = np.exp2(byte - 127.0)
    codes = (blocks / scale).astype(np.float32).astype(dtype).astype(np.float64)
    return np.moveaxis((codes * scale).reshape(v.shape), -1, axis)


WIDE = False


def mx_kscale(k):
    if not WIDE:
        return np.ones(k)
    levels = np.array([10, -10, 5, -5, 0])
    if k % 512:
        return np.exp2(np.random.permutation(np.resize(levels, k // 32))).repeat(32)
    a = np.empty((k // 512, 16))
    for p in range(k // 512):
        a[p, :8] = np.random.permutation(np.resize(levels, 8))
        for g in range(8):
            far = levels[np.abs(levels - a[p, g]) >= 10]
            a[p, g + 8] = far[np.random.randint(len(far))]
    return np.exp2(a.ravel()).repeat(32)


def f64(x):
    return np.asarray(x).astype(np.float64)


def striped8(idx):
    return np.asarray(idx).reshape(8, -1, 16).transpose(0, 2, 1).reshape(128, -1).astype(np.uint16)


def unstriped8(offs):
    return offs.reshape(8, 16, -1).transpose(0, 2, 1).reshape(8, -1).astype(np.int64)


def pick8(x, idx, run):
    r = np.arange(len(x))
    return x[r[:, None], idx[r % (8 * run) // run]]


E2M1 = np.array([0.0, 0.5, 1.0, 1.5, 2.0, 3.0, 4.0, 6.0, -0.0, -0.5, -1.0, -1.5, -2.0, -3.0, -4.0, -6.0])


def pack_weight(w, fmt):
    k, n = w.shape
    w = f64(np.asarray(w, np.float32).astype(ml_dtypes.bfloat16)).reshape(k // 32, 32, n)
    amax = np.abs(w).max(1)
    if fmt == "e4m3":
        byte = np.frexp(amax)[1] - 1 + 127 - 7
    else:
        mant, ex = np.frexp(amax / 6.0)
        byte = np.where(mant > 0.5, ex, ex - 1) + 127
    byte = np.clip(np.where(amax > 0, byte, 1), 1, 254)
    scaled = (w * np.exp2(127.0 - byte)[:, None, :]).reshape(k, n).astype(np.float32)
    by_word = np.ascontiguousarray(scaled.reshape(k // 512, 128, 4, n).transpose(0, 1, 3, 2))
    if fmt == "e4m3":
        words = by_word.astype(ml_dtypes.float8_e4m3fn).view(np.uint8)
    else:
        c = by_word.astype(ml_dtypes.float4_e2m1fn).view(np.uint8) & 0xF
        words = (c[..., 0::2] | (c[..., 1::2] << 4)).reshape(k // 512, 128, 2 * n)
    return np.ascontiguousarray(words), np.ascontiguousarray(byte.astype(np.uint8).reshape(k // 512, 16, n))


def unpack_weight(words, scales, fmt):
    g, _, n = scales.shape
    words = np.ascontiguousarray(words).reshape(g, 128, n, -1)
    if fmt == "e4m3":
        vals = words.view(ml_dtypes.float8_e4m3fn).astype(np.float64)
    else:
        nib = np.empty((g, 128, n, 4), np.uint8)
        nib[..., 0::2] = words & 0xF
        nib[..., 1::2] = words >> 4
        vals = E2M1[nib]
    vals = vals * np.repeat(np.exp2(scales.astype(np.float64) - 127.0), 8, axis=1)[..., None]
    return vals.transpose(0, 1, 3, 2).reshape(g * 512, n)


D, V, Q, I = 512, 2048, 128, 512


def setup_inputs():
    n = np.random.standard_normal
    idx = np.stack([np.random.permutation(V)[:I] for _ in range(8)])
    fd = mx_kscale(D)
    vocp = pack_weight(n((D, V)) / fd[:, None], "e4m3")
    return {
        "hid": (n((D, Q)) * 1.0 / np.sqrt(D) * fd[:, None]).astype(np.float32),
        "voc_words": vocp[0],
        "voc_scales": vocp[1],
        "sw": (np.random.uniform(0.5, 2.0, (1, I))).astype(np.float32),
        "old": (0.5 * n((Q, V))).astype(np.float32),
        "offs": striped8(idx),
    }


def reference(hid, voc_words, voc_scales, sw, old, offs):
    idx = unstriped8(offs)
    vocu = unpack_weight(voc_words, voc_scales, "e4m3")
    hidq = mxq(f64(hid), 0, "e4m3")
    a = hidq.T @ vocu
    m1 = np.max(a, axis=1, keepdims=True)
    px = np.exp(pick8(a, idx, 16) - m1)
    zl = np.sum(px, axis=1, keepdims=True)
    dzl = np.sum(f64(sw) / (px / zl + 0.001) * px / np.square(zl) * (-1.0), axis=1, keepdims=True)
    dpx = f64(sw) / (px / zl + 0.001) / zl + dzl
    e1 = dpx * px
    s1 = np.zeros((Q, V))
    s1[np.arange(Q)[:, None], idx[np.arange(Q) % 128 // 16]] = e1
    y = s1 + f64(old)
    return y

@@ -1,0 +1,167 @@
+import math
+from contextlib import ExitStack
+
+import concourse.mybir as mybir
+from concourse.masks import make_identity
+
+F32 = mybir.dt.float32
+BF16 = mybir.dt.bfloat16
+I32 = mybir.dt.int32
+U32 = mybir.dt.uint32
+U16 = mybir.dt.uint16
+U8 = mybir.dt.uint8
+FP8X4 = mybir.dt.float8_e4m3fn_x4
+ALU = mybir.AluOpType
+ACT = mybir.ActivationFunctionType
+AX = mybir.AxisListType
+
+P = 128
+D, V, Q, SLOTS = 512, 2048, 128, 512
+PACK = 4
+BLOCK = 512
+EPS = 0.001
+FLOPS = 2 * D * V * Q
+
+SCORE_WIDTHS = (256, 256, 512, 512, 512)
+STORE_WIDTHS = (256, 512, 512, 512, 256)
+
+BITS_TO_LN = math.log(2.0) / 2.0**23
+GUESS_SHIFT = 88.0
+TERMS = 16
+
+
+def tile_attend_blistshare_heads_kernel(tc, hid, voc_words, voc_scales, sw, old, offs, out):
+    nc = tc.nc
+    with ExitStack() as ctx:
+        keep = ctx.enter_context(tc.tile_pool(name="keep", bufs=1))
+        psum = ctx.enter_context(tc.psum_pool(name="psum", bufs=1))
+
+        planes = keep.tile([P, BLOCK], U8, name="planes", align_bytes=64)
+        nc.vector.memset(planes[:].bitcast(I32), 0)
+
+        hid_raw = keep.tile([P, PACK, Q], F32, name="hid_raw")
+        nc.sync.dma_start(out=hid_raw[:], in_=hid.rearrange("(p t) q -> p t q", t=PACK))
+        sw_cols = keep.tile([P, PACK], F32, name="sw_cols")
+        nc.scalar.dma_start(out=sw_cols[:], in_=sw[0].rearrange("(p t) -> p t", t=PACK))
+        for quad in range(4):
+            rows = voc_scales[0, 4 * quad : 4 * quad + 4, :].rearrange("r (j c) -> j r c", c=BLOCK)
+            nc.sync.dma_start(out=planes[32 * quad : 32 * quad + 16, :].bitcast(I32), in_=rows.bitcast(I32))
+        flat_words = voc_words[0].rearrange("p n t -> p (n t)")
+        words = []
+        for j in range(V // BLOCK):
+            block = keep.tile([P, BLOCK], U32, name=f"words{j}", align_bytes=64)
+            nc.sync.dma_start(
+                out=block[:].bitcast(I32),
+                in_=flat_words[:, j * BLOCK * PACK : (j + 1) * BLOCK * PACK].bitcast(I32),
+            )
+            words.append(block)
+        offsets = keep.tile([P, SLOTS // 16], U16, name="offsets")
+        nc.sync.dma_start(offsets[:], offs)
+        old_sb = keep.tile([P, V], F32, name="old_sb")
+        nc.sync.dma_start(out=old_sb[:], in_=old)
+
+        ident = keep.tile([P, P], F32, name="ident")
+        make_identity(nc, ident[:])
+        evens = keep.tile([P, TERMS], F32, name="evens")
+        nc.gpsimd.iota(
+            evens[:], [[-2, TERMS]], base=2 * TERMS, channel_multiplier=0, allow_small_or_imprecise_dtypes=True
+        )
+        shift = keep.tile([P, 1], F32, name="shift")
+        nc.gpsimd.memset(shift[:], GUESS_SHIFT)
+
+        placed = keep.tile([P, V], F32, name="placed")
+        nc.vector.memset(placed[:], 0.0)
+        addends = keep.tile([P, TERMS + 1], F32, name="addends")
+        nc.vector.reciprocal(addends[:, 0:TERMS], evens[:])
+
+        sw_bank = psum.tile([P, PACK, P], F32, name="sw_bank")
+        for t in range(PACK):
+            nc.tensor.transpose(sw_bank[:, t, :], sw_cols[:, t : t + 1].to_broadcast([P, P]), ident[:])
+        half_sw = keep.tile([P, SLOTS], F32, name="half_sw")
+        nc.scalar.activation(
+            half_sw[:].rearrange("q (p t) -> q p t", t=PACK), sw_bank[:].rearrange("q t p -> q p t"), ACT.Copy, scale=0.5
+        )
+
+        hid_bf = keep.tile([P, Q, PACK], BF16, name="hid_bf", align_bytes=64)
+        nc.vector.tensor_copy(
+            out=hid_bf[:].rearrange("p (c i) t -> p c t i", i=4),
+            in_=hid_raw[:].rearrange("p t (c i) -> p c t i", i=4),
+        )
+        hid_codes = keep.tile([P, Q], U32, name="hid_codes", align_bytes=64)
+        hid_scales = keep.tile([P, Q], U8, name="hid_scales", align_bytes=64)
+        nc.vector.quantize_mx(
+            out=hid_codes[:].bitcast(FP8X4), scales=hid_scales[:], in_=hid_bf[:].rearrange("p q t -> p (q t)")
+        )
+
+        scores = keep.tile([P, V], F32, name="scores")
+        piece_max = keep.tile([P, len(SCORE_WIDTHS)], F32, name="piece_max")
+        first = 0
+        for n, width in enumerate(SCORE_WIDTHS):
+            j, c0 = divmod(first, BLOCK)
+            bank = psum.tile([P, width], F32, name=f"bank{n}")
+            nc.tensor.matmul_mx(
+                out=bank[:],
+                lhsT=hid_codes[:].bitcast(FP8X4),
+                lhsT_scale=hid_scales[:],
+                rhs=words[j][:, c0 : c0 + width].bitcast(FP8X4),
+                rhs_scale=planes[4 * j : P, c0 : c0 + width],
+                start=True,
+                stop=True,
+            )
+            nc.vector.tensor_scalar(
+                scores[:, first : first + width], bank[:], 1.0, None, ALU.mult, ALU.max,
+                accum_out=piece_max[:, n : n + 1],
+            )
+            first = first + width
+        neg_max = keep.tile([P, 1], F32, name="neg_max")
+        nc.vector.tensor_reduce(neg_max[:], piece_max[:], AX.X, ALU.max, negate=True)
+
+        px = keep.tile([P, SLOTS], F32, name="px")
+        zl = keep.tile([P, 1], F32, name="zl")
+        listed = keep.tile([P, SLOTS], F32, name="listed")
+        nc.vector.tensor_copy(listed[:], scores[:].indirect(offsets[:]))
+        nc.scalar.activation(px[:], listed[:], ACT.Exp, bias=neg_max[:], accum_out=zl[:])
+        row_term = keep.tile([P, 1], F32, name="row_term")
+        nc.vector.tensor_scalar(
+            row_term[:], neg_max[:], 0.5,
+            0.5 * (GUESS_SHIFT - math.log(EPS)), ALU.mult, ALU.add,
+        )
+
+        inv_guess = keep.tile([P, 1], F32, name="inv_guess")
+        nc.scalar.activation(inv_guess[:], zl[:].bitcast(U32), ACT.Exp, bias=shift[:], scale=-BITS_TO_LN)
+        neg_zl = keep.tile([P, 1], F32, name="neg_zl")
+        nc.vector.tensor_scalar(neg_zl[:], zl[:], -1.0, None, ALU.mult)
+        nc.vector.tensor_scalar(
+            addends[:, TERMS : TERMS + 1], zl[:].bitcast(I32), -0.5 * BITS_TO_LN, row_term[:], ALU.mult, ALU.add
+        )
+        miss = keep.tile([P, TERMS + 1], F32, name="miss")
+        nc.vector.tensor_scalar(
+            miss[:], inv_guess[:].to_broadcast([P, TERMS + 1]), neg_zl[:], 1.0, ALU.mult, ALU.add
+        )
+        horner = keep.tile([P, TERMS + 1], F32, name="horner")
+        nc.vector.tensor_tensor_scan(horner[:], miss[:], addends[:], 0.0, ALU.mult, ALU.add)
+        tanh = keep.tile([P, SLOTS], F32, name="tanh")
+        nc.scalar.activation(tanh[:], listed[:], ACT.Tanh, bias=horner[:, TERMS : TERMS + 1], scale=0.5)
+
+        inv_zl = keep.tile([P, 1], F32, name="inv_zl")
+        nc.vector.reciprocal(inv_zl[:], zl[:])
+        neg_share = keep.tile([P, SLOTS], F32, name="neg_share")
+        nc.vector.tensor_scalar(neg_share[:], px[:], inv_zl[:], -1.0, ALU.mult, ALU.mult)
+
+        direct = keep.tile([P, SLOTS], F32, name="direct")
+        total = keep.tile([P, 1], F32, name="total")
+        nc.vector.scalar_tensor_tensor(
+            direct[:], tanh[:], 1.0, half_sw[:], ALU.add, ALU.mult, accum_out=total[:]
+        )
+        through_sum = keep.tile([P, SLOTS], F32, name="through_sum")
+        nc.vector.tensor_scalar(through_sum[:], neg_share[:], total[:], None, ALU.mult)
+        nc.vector.tensor_tensor(placed[:].indirect(offsets[:]), direct[:], through_sum[:], ALU.add)
+
+        first = 0
+        for n, width in enumerate(STORE_WIDTHS):
+            cols = slice(first, first + width)
+            result = keep.tile([P, width], F32, name=f"result{n}")
+            nc.vector.tensor_tensor(result[:], placed[:, cols], old_sb[:, cols], ALU.add)
+            queue = nc.sync if n % 2 == 0 else nc.scalar
+            queue.dma_start(out=out[:, cols], in_=result[:])
+            first = first + width

@@ -22,6 +22,7 @@ BLOCK = 512
 EPS = 0.001
 FLOPS = 2 * D * V * Q
 
+LOAD_WIDTHS = (512, 512, 512, 512)
 SCORE_WIDTHS = (256, 256, 512, 512, 512)
 STORE_WIDTHS = (256, 512, 512, 512, 256)
 
@@ -41,64 +42,66 @@ def tile_attend_blistshare_heads_kernel(tc, hid, voc_words, voc_scales, sw, old,
 
         hid_raw = keep.tile([P, PACK, Q], F32, name="hid_raw")
         nc.sync.dma_start(out=hid_raw[:], in_=hid.rearrange("(p t) q -> p t q", t=PACK))
-        sw_cols = keep.tile([P, PACK], F32, name="sw_cols")
-        nc.scalar.dma_start(out=sw_cols[:], in_=sw[0].rearrange("(p t) -> p t", t=PACK))
         for quad in range(4):
             rows = voc_scales[0, 4 * quad : 4 * quad + 4, :].rearrange("r (j c) -> j r c", c=BLOCK)
             nc.sync.dma_start(out=planes[32 * quad : 32 * quad + 16, :].bitcast(I32), in_=rows.bitcast(I32))
         flat_words = voc_words[0].rearrange("p n t -> p (n t)")
         words = []
-        for j in range(V // BLOCK):
-            block = keep.tile([P, BLOCK], U32, name=f"words{j}", align_bytes=64)
+        first = 0
+        for n, width in enumerate(LOAD_WIDTHS):
+            loaded = keep.tile([P, width], U32, name=f"words{n}", align_bytes=64)
             nc.sync.dma_start(
-                out=block[:].bitcast(I32),
-                in_=flat_words[:, j * BLOCK * PACK : (j + 1) * BLOCK * PACK].bitcast(I32),
+                out=loaded[:].bitcast(I32),
+                in_=flat_words[:, first * PACK : (first + width) * PACK].bitcast(I32),
             )
-            words.append(block)
+            words.extend(loaded[:, c : c + BLOCK] for c in range(0, width, BLOCK))
+            first = first + width
         offsets = keep.tile([P, SLOTS // 16], U16, name="offsets")
         nc.sync.dma_start(offsets[:], offs)
+        sw_cols = keep.tile([P, PACK], F32, name="sw_cols")
+        nc.sync.dma_start(out=sw_cols[:], in_=sw[0].rearrange("(p t) -> p t", t=PACK))
         old_sb = keep.tile([P, V], F32, name="old_sb")
         nc.sync.dma_start(out=old_sb[:], in_=old)
 
-        ident = keep.tile([P, P], F32, name="ident")
-        make_identity(nc, ident[:])
         evens = keep.tile([P, TERMS], F32, name="evens")
         nc.gpsimd.iota(
             evens[:], [[-2, TERMS]], base=2 * TERMS, channel_multiplier=0, allow_small_or_imprecise_dtypes=True
         )
         shift = keep.tile([P, 1], F32, name="shift")
-        nc.gpsimd.memset(shift[:], GUESS_SHIFT)
+        nc.vector.memset(shift[:], GUESS_SHIFT)
 
         placed = keep.tile([P, V], F32, name="placed")
         nc.vector.memset(placed[:], 0.0)
         addends = keep.tile([P, TERMS + 1], F32, name="addends")
         nc.vector.reciprocal(addends[:, 0:TERMS], evens[:])
 
-        sw_bank = psum.tile([P, PACK, P], F32, name="sw_bank")
-        for t in range(PACK):
-            nc.tensor.transpose(sw_bank[:, t, :], sw_cols[:, t : t + 1].to_broadcast([P, P]), ident[:])
-        half_sw = keep.tile([P, SLOTS], F32, name="half_sw")
-        nc.scalar.activation(
-            half_sw[:].rearrange("q (p t) -> q p t", t=PACK), sw_bank[:].rearrange("q t p -> q p t"), ACT.Copy, scale=0.5
-        )
-
-        hid_bf = keep.tile([P, Q, PACK], BF16, name="hid_bf", align_bytes=64)
-        nc.vector.tensor_copy(
-            out=hid_bf[:].rearrange("p (c i) t -> p c t i", i=4),
-            in_=hid_raw[:].rearrange("p t (c i) -> p c t i", i=4),
-        )
+        halves = [slice(0, Q // 2), slice(Q // 2, Q)]
+        hid_bf = [
+            keep.tile([P, Q // 2, PACK], BF16, name=f"hid_bf{h}", tag=f"hid_bf{h}", align_bytes=64) for h in range(2)
+        ]
+        for rounded, rows in zip(hid_bf, halves):
+            nc.vector.tensor_copy(
+                out=rounded[:].rearrange("p (c i) t -> p c t i", i=4),
+                in_=hid_raw[:, :, rows].rearrange("p t (c i) -> p c t i", i=4),
+            )
         hid_codes = keep.tile([P, Q], U32, name="hid_codes", align_bytes=64)
         hid_scales = keep.tile([P, Q], U8, name="hid_scales", align_bytes=64)
-        nc.vector.quantize_mx(
-            out=hid_codes[:].bitcast(FP8X4), scales=hid_scales[:], in_=hid_bf[:].rearrange("p q t -> p (q t)")
-        )
+        for rounded, rows in zip(hid_bf, halves):
+            nc.vector.quantize_mx(
+                out=hid_codes[:, rows].bitcast(FP8X4),
+                scales=hid_scales[:, rows],
+                in_=rounded[:].rearrange("p q t -> p (q t)"),
+            )
+
+        ident = keep.tile([P, P], F32, name="ident", tag="hid_bf1", align_bytes=64)
+        make_identity(nc, ident[:])
 
         scores = keep.tile([P, V], F32, name="scores")
         piece_max = keep.tile([P, len(SCORE_WIDTHS)], F32, name="piece_max")
         first = 0
         for n, width in enumerate(SCORE_WIDTHS):
             j, c0 = divmod(first, BLOCK)
-            bank = psum.tile([P, width], F32, name=f"bank{n}")
+            bank = psum.tile([P, width], F32, name=f"bank{n}", tag=f"bank{n}")
             nc.tensor.matmul_mx(
                 out=bank[:],
                 lhsT=hid_codes[:].bitcast(FP8X4),
@@ -115,6 +118,12 @@ def tile_attend_blistshare_heads_kernel(tc, hid, voc_words, voc_scales, sw, old,
             first = first + width
         neg_max = keep.tile([P, 1], F32, name="neg_max")
         nc.vector.tensor_reduce(neg_max[:], piece_max[:], AX.X, ALU.max, negate=True)
+
+        half_cols = keep.tile([P, PACK], F32, name="half_cols")
+        nc.scalar.activation(half_cols[:], sw_cols[:], ACT.Copy, scale=0.5)
+        half_sw = psum.tile([P, PACK, P], F32, name="half_sw", tag="bank3")
+        for t in range(PACK):
+            nc.tensor.transpose(half_sw[:, t, :], half_cols[:, t : t + 1].to_broadcast([P, P]), ident[:])
 
         px = keep.tile([P, SLOTS], F32, name="px")
         zl = keep.tile([P, 1], F32, name="zl")
@@ -143,18 +152,22 @@ def tile_attend_blistshare_heads_kernel(tc, hid, voc_words, voc_scales, sw, old,
         tanh = keep.tile([P, SLOTS], F32, name="tanh")
         nc.scalar.activation(tanh[:], listed[:], ACT.Tanh, bias=horner[:, TERMS : TERMS + 1], scale=0.5)
 
-        inv_zl = keep.tile([P, 1], F32, name="inv_zl")
-        nc.vector.reciprocal(inv_zl[:], zl[:])
-        neg_share = keep.tile([P, SLOTS], F32, name="neg_share")
-        nc.vector.tensor_scalar(neg_share[:], px[:], inv_zl[:], -1.0, ALU.mult, ALU.mult)
+        neg_inv_zl = keep.tile([P, 1], F32, name="neg_inv_zl")
+        nc.vector.reciprocal(neg_inv_zl[:], neg_zl[:])
 
         direct = keep.tile([P, SLOTS], F32, name="direct")
         total = keep.tile([P, 1], F32, name="total")
         nc.vector.scalar_tensor_tensor(
-            direct[:], tanh[:], 1.0, half_sw[:], ALU.add, ALU.mult, accum_out=total[:]
+            direct[:].rearrange("q (p t) -> q p t", t=PACK),
+            tanh[:].rearrange("q (p t) -> q p t", t=PACK),
+            1.0,
+            half_sw[:].rearrange("q t p -> q p t"),
+            ALU.add,
+            ALU.mult,
+            accum_out=total[:],
         )
         through_sum = keep.tile([P, SLOTS], F32, name="through_sum")
-        nc.vector.tensor_scalar(through_sum[:], neg_share[:], total[:], None, ALU.mult)
+        nc.vector.tensor_scalar(through_sum[:], px[:], total[:], neg_inv_zl[:], ALU.mult, ALU.mult)
         nc.vector.tensor_tensor(placed[:].indirect(offsets[:]), direct[:], through_sum[:], ALU.add)
 
         first = 0

import math
from contextlib import ExitStack

import concourse.mybir as mybir
from concourse.masks import make_identity

F32 = mybir.dt.float32
BF16 = mybir.dt.bfloat16
I32 = mybir.dt.int32
U32 = mybir.dt.uint32
U16 = mybir.dt.uint16
U8 = mybir.dt.uint8
FP8X4 = mybir.dt.float8_e4m3fn_x4
ALU = mybir.AluOpType
ACT = mybir.ActivationFunctionType
AX = mybir.AxisListType

P = 128
D, V, Q, SLOTS = 512, 2048, 128, 512
PACK = 4
BLOCK = 512
EPS = 0.001
FLOPS = 2 * D * V * Q

LOAD_WIDTHS = (512, 512, 512, 512)
SCORE_WIDTHS = (256, 256, 512, 512, 512)
STORE_WIDTHS = (256, 512, 512, 512, 256)

BITS_TO_LN = math.log(2.0) / 2.0**23
GUESS_SHIFT = 88.0
TERMS = 16


def tile_attend_blistshare_heads_kernel(tc, hid, voc_words, voc_scales, sw, old, offs, out):
    nc = tc.nc
    with ExitStack() as ctx:
        keep = ctx.enter_context(tc.tile_pool(name="keep", bufs=1))
        psum = ctx.enter_context(tc.psum_pool(name="psum", bufs=1))

        planes = keep.tile([P, BLOCK], U8, name="planes", align_bytes=64)
        nc.vector.memset(planes[:].bitcast(I32), 0)

        hid_raw = keep.tile([P, PACK, Q], F32, name="hid_raw")
        nc.sync.dma_start(out=hid_raw[:], in_=hid.rearrange("(p t) q -> p t q", t=PACK))
        for quad in range(4):
            rows = voc_scales[0, 4 * quad : 4 * quad + 4, :].rearrange("r (j c) -> j r c", c=BLOCK)
            nc.sync.dma_start(out=planes[32 * quad : 32 * quad + 16, :].bitcast(I32), in_=rows.bitcast(I32))
        flat_words = voc_words[0].rearrange("p n t -> p (n t)")
        words = []
        first = 0
        for n, width in enumerate(LOAD_WIDTHS):
            loaded = keep.tile([P, width], U32, name=f"words{n}", align_bytes=64)
            nc.sync.dma_start(
                out=loaded[:].bitcast(I32),
                in_=flat_words[:, first * PACK : (first + width) * PACK].bitcast(I32),
            )
            words.extend(loaded[:, c : c + BLOCK] for c in range(0, width, BLOCK))
            first = first + width
        offsets = keep.tile([P, SLOTS // 16], U16, name="offsets")
        nc.sync.dma_start(offsets[:], offs)
        sw_cols = keep.tile([P, PACK], F32, name="sw_cols")
        nc.sync.dma_start(out=sw_cols[:], in_=sw[0].rearrange("(p t) -> p t", t=PACK))
        old_sb = keep.tile([P, V], F32, name="old_sb")
        nc.sync.dma_start(out=old_sb[:], in_=old)

        evens = keep.tile([P, TERMS], F32, name="evens")
        nc.gpsimd.iota(
            evens[:], [[-2, TERMS]], base=2 * TERMS, channel_multiplier=0, allow_small_or_imprecise_dtypes=True
        )
        shift = keep.tile([P, 1], F32, name="shift")
        nc.vector.memset(shift[:], GUESS_SHIFT)

        placed = keep.tile([P, V], F32, name="placed")
        nc.vector.memset(placed[:], 0.0)
        addends = keep.tile([P, TERMS + 1], F32, name="addends")
        nc.vector.reciprocal(addends[:, 0:TERMS], evens[:])

        halves = [slice(0, Q // 2), slice(Q // 2, Q)]
        hid_bf = [
            keep.tile([P, Q // 2, PACK], BF16, name=f"hid_bf{h}", tag=f"hid_bf{h}", align_bytes=64) for h in range(2)
        ]
        for rounded, rows in zip(hid_bf, halves):
            nc.vector.tensor_copy(
                out=rounded[:].rearrange("p (c i) t -> p c t i", i=4),
                in_=hid_raw[:, :, rows].rearrange("p t (c i) -> p c t i", i=4),
            )
        hid_codes = keep.tile([P, Q], U32, name="hid_codes", align_bytes=64)
        hid_scales = keep.tile([P, Q], U8, name="hid_scales", align_bytes=64)
        for rounded, rows in zip(hid_bf, halves):
            nc.vector.quantize_mx(
                out=hid_codes[:, rows].bitcast(FP8X4),
                scales=hid_scales[:, rows],
                in_=rounded[:].rearrange("p q t -> p (q t)"),
            )

        ident = keep.tile([P, P], F32, name="ident", tag="hid_bf1", align_bytes=64)
        make_identity(nc, ident[:])

        scores = keep.tile([P, V], F32, name="scores")
        piece_max = keep.tile([P, len(SCORE_WIDTHS)], F32, name="piece_max")
        first = 0
        for n, width in enumerate(SCORE_WIDTHS):
            j, c0 = divmod(first, BLOCK)
            bank = psum.tile([P, width], F32, name=f"bank{n}", tag=f"bank{n}")
            nc.tensor.matmul_mx(
                out=bank[:],
                lhsT=hid_codes[:].bitcast(FP8X4),
                lhsT_scale=hid_scales[:],
                rhs=words[j][:, c0 : c0 + width].bitcast(FP8X4),
                rhs_scale=planes[4 * j : P, c0 : c0 + width],
                start=True,
                stop=True,
            )
            nc.vector.tensor_scalar(
                scores[:, first : first + width], bank[:], 1.0, None, ALU.mult, ALU.max,
                accum_out=piece_max[:, n : n + 1],
            )
            first = first + width
        neg_max = keep.tile([P, 1], F32, name="neg_max")
        nc.vector.tensor_reduce(neg_max[:], piece_max[:], AX.X, ALU.max, negate=True)

        half_cols = keep.tile([P, PACK], F32, name="half_cols")
        nc.scalar.activation(half_cols[:], sw_cols[:], ACT.Copy, scale=0.5)
        half_sw = psum.tile([P, PACK, P], F32, name="half_sw", tag="bank3")
        for t in range(PACK):
            nc.tensor.transpose(half_sw[:, t, :], half_cols[:, t : t + 1].to_broadcast([P, P]), ident[:])

        px = keep.tile([P, SLOTS], F32, name="px")
        zl = keep.tile([P, 1], F32, name="zl")
        listed = keep.tile([P, SLOTS], F32, name="listed")
        nc.vector.tensor_copy(listed[:], scores[:].indirect(offsets[:]))
        nc.scalar.activation(px[:], listed[:], ACT.Exp, bias=neg_max[:], accum_out=zl[:])
        row_term = keep.tile([P, 1], F32, name="row_term")
        nc.vector.tensor_scalar(
            row_term[:], neg_max[:], 0.5,
            0.5 * (GUESS_SHIFT - math.log(EPS)), ALU.mult, ALU.add,
        )

        inv_guess = keep.tile([P, 1], F32, name="inv_guess")
        nc.scalar.activation(inv_guess[:], zl[:].bitcast(U32), ACT.Exp, bias=shift[:], scale=-BITS_TO_LN)
        neg_zl = keep.tile([P, 1], F32, name="neg_zl")
        nc.vector.tensor_scalar(neg_zl[:], zl[:], -1.0, None, ALU.mult)
        nc.vector.tensor_scalar(
            addends[:, TERMS : TERMS + 1], zl[:].bitcast(I32), -0.5 * BITS_TO_LN, row_term[:], ALU.mult, ALU.add
        )
        miss = keep.tile([P, TERMS + 1], F32, name="miss")
        nc.vector.tensor_scalar(
            miss[:], inv_guess[:].to_broadcast([P, TERMS + 1]), neg_zl[:], 1.0, ALU.mult, ALU.add
        )
        horner = keep.tile([P, TERMS + 1], F32, name="horner")
        nc.vector.tensor_tensor_scan(horner[:], miss[:], addends[:], 0.0, ALU.mult, ALU.add)
        tanh = keep.tile([P, SLOTS], F32, name="tanh")
        nc.scalar.activation(tanh[:], listed[:], ACT.Tanh, bias=horner[:, TERMS : TERMS + 1], scale=0.5)

        neg_inv_zl = keep.tile([P, 1], F32, name="neg_inv_zl")
        nc.vector.reciprocal(neg_inv_zl[:], neg_zl[:])

        direct = keep.tile([P, SLOTS], F32, name="direct")
        total = keep.tile([P, 1], F32, name="total")
        nc.vector.scalar_tensor_tensor(
            direct[:].rearrange("q (p t) -> q p t", t=PACK),
            tanh[:].rearrange("q (p t) -> q p t", t=PACK),
            1.0,
            half_sw[:].rearrange("q t p -> q p t"),
            ALU.add,
            ALU.mult,
            accum_out=total[:],
        )
        through_sum = keep.tile([P, SLOTS], F32, name="through_sum")
        nc.vector.tensor_scalar(through_sum[:], px[:], total[:], neg_inv_zl[:], ALU.mult, ALU.mult)
        nc.vector.tensor_tensor(placed[:].indirect(offsets[:]), direct[:], through_sum[:], ALU.add)

        first = 0
        for n, width in enumerate(STORE_WIDTHS):
            cols = slice(first, first + width)
            result = keep.tile([P, width], F32, name=f"result{n}")
            nc.vector.tensor_tensor(result[:], placed[:, cols], old_sb[:, cols], ALU.add)
            queue = nc.sync if n % 2 == 0 else nc.scalar
            queue.dma_start(out=out[:, cols], in_=result[:])
            first = first + width
